import numpy as np
import ml_dtypes


def mxq(x, axis, fmt="e4m3"):
    dtype, down = {"e4m3": (ml_dtypes.float8_e4m3fn, 7), "e5m2": (ml_dtypes.float8_e5m2, 14)}[fmt]
    v = np.moveaxis(np.asarray(x, np.float32).astype(ml_dtypes.bfloat16).astype(np.float64), axis, -1)
    blocks = v.reshape(v.shape[:-1] + (-1, 32))
    amax = np.abs(blocks).max(-1, keepdims=True)
    byte = np.maximum(np.where(amax > 0, np.frexp(amax)[1] - 1 + 127, 0) - down, 1)
    scale = np.exp2(byte - 127.0)
    codes = (blocks / scale).astype(np.float32).astype(dtype).astype(np.float64)
    return np.moveaxis((codes * scale).reshape(v.shape), -1, axis)


WIDE = False


def mx_kscale(k):
    if not WIDE:
        return np.ones(k)
    levels = np.array([10, -10, 5, -5, 0])
    if k % 512:
        return np.exp2(np.random.permutation(np.resize(levels, k // 32))).repeat(32)
    a = np.empty((k // 512, 16))
    for p in range(k // 512):
        a[p, :8] = np.random.permutation(np.resize(levels, 8))
        for g in range(8):
            far = levels[np.abs(levels - a[p, g]) >= 10]
            a[p, g + 8] = far[np.random.randint(len(far))]
    return np.exp2(a.ravel()).repeat(32)


def f64(x):
    return np.asarray(x).astype(np.float64)


def striped(idx):
    return np.tile(idx.reshape(-1, 16).T, (8, 1)).astype(np.uint16)


def unstriped(offs):
    return offs[:16].T.reshape(-1).astype(np.int64)


def pack_weight(w):
    k, n = w.shape
    w = f64(np.asarray(w, np.float32).astype(ml_dtypes.bfloat16)).reshape(k // 32, 32, n)
    amax = np.abs(w).max(1)
    byte = np.clip(np.where(amax > 0, np.frexp(amax)[1] - 1 + 127 - 7, 1), 1, 254)
    scaled = (w * np.exp2(127.0 - byte)[:, None, :]).reshape(k, n).astype(np.float32)
    words = np.ascontiguousarray(scaled.reshape(k // 512, 128, 4, n).transpose(0, 1, 3, 2)).astype(ml_dtypes.float8_e4m3fn).view(np.uint8)
    return words, np.ascontiguousarray(byte.astype(np.uint8).reshape(k // 512, 16, n))


def unpack_weight(words, scales):
    g, p, n, _ = words.shape
    vals = np.ascontiguousarray(words).view(ml_dtypes.float8_e4m3fn).astype(np.float64) * np.repeat(np.exp2(scales.astype(np.float64) - 127.0), 8, axis=1)[..., None]
    return vals.transpose(0, 1, 3, 2).reshape(g * 512, n)


def planes(y):
    n, m = y.shape
    v = y.astype(np.float32).astype(ml_dtypes.bfloat16).astype(np.float64).reshape(n // 32, 32, m)
    top = np.abs(v).max(1)
    byte = np.clip(np.where(top > 0, np.frexp(top)[1] - 1 + 127 - 7, 1), 1, 254)
    codes = (v * np.exp2(127.0 - byte)[:, None, :]).reshape(n, m).astype(np.float32).astype(ml_dtypes.float8_e4m3fn).view(np.uint8)
    words = codes.reshape(n // 512, 128, 4, m).transpose(0, 1, 3, 2)
    return np.ascontiguousarray(words), np.ascontiguousarray(byte.astype(np.uint8).reshape(n // 512, 16, m))


def gelu(v):
    return 0.5 * v * (1.0 + np.tanh(np.sqrt(2.0 / np.pi) * (v + 0.044715 * v**3)))


K, T, S, D, V, H, N = 512, 1024, 512, 2, 256, 512, 512
P = 2 ** 7


def setup_inputs():
    n = np.random.standard_normal
    s = mx_kscale(K)[:, None]
    u = mx_kscale(H)
    near = np.random.permutation(S)
    packed_xT = pack_weight(n((K, T)) * s)
    return {
        "x_words": packed_xT[0],
        "x_scales": packed_xT[1],
        "w1": (n((K, H)) / np.sqrt(K) / s * u).astype(np.float32),
        "w2": (n((H, N)) / np.sqrt(2 * H) / u[:, None]).astype(np.float32),
        "gate": (np.tile(np.random.uniform(0.2, 1.0, (D, 1, V)) / np.sqrt(D), (1, P, 1))).astype(np.float32),
        "eT": (n((K, V)) * s).astype(np.float32),
        "w3": (n((K, N)) / np.sqrt(2 * K) / s).astype(np.float32),
        "offs": striped(np.random.permutation(T)[:S]),
        "pos1": striped(near[:V]),
        "pos2": striped(near[V:]),
    }


def reference(x_words, x_scales, w1, w2, gate, eT, w3, offs, pos1, pos2):
    xq = unpack_weight(x_words, x_scales)[:, unstriped(offs)]
    h = gelu(mxq(f64(w1), 0, "e4m3").T @ xq)
    z = h[:, unstriped(pos1)] * f64(gate)[0, :1] + h[:, unstriped(pos2)] * f64(gate)[1, :1]
    eTq = mxq(f64(eT), 0, "e4m3")
    out_0 = gelu(mxq(f64(w2), 0, "e4m3").T @ mxq(z, 0, "e4m3") + mxq(f64(w3), 0, "e4m3").T @ eTq)
    return (out_0,) + planes(out_0)

@@ -1,0 +1,199 @@
+from contextlib import ExitStack
+
+import concourse.mybir as mybir
+
+K, T, S, V, H, N = 512, 1024, 512, 256, 512, 512
+FLOPS = 2 * K * H * S + 2 * H * N * V + 2 * K * N * V
+
+F32 = mybir.dt.float32
+BF16 = mybir.dt.bfloat16
+I32 = mybir.dt.int32
+U32 = mybir.dt.uint32
+U16 = mybir.dt.uint16
+U8 = mybir.dt.uint8
+FP8X4 = mybir.dt.float8_e4m3fn_x4
+GELU = mybir.ActivationFunctionType.Gelu_apprx_tanh
+MULT = mybir.AluOpType.mult
+ADD = mybir.AluOpType.add
+
+P = 128
+PACK = 4
+HALF_V = V // 2
+W1_VECTOR_M = 40
+W2_VECTOR_M = 32
+
+
+def tile_picked_zfp_gelu_po_kernel(
+    tc, x_words, x_scales, w1, w2, gate, eT, w3, offs, pos1, pos2, out_0, out_1, out_2
+):
+    nc = tc.nc
+    with ExitStack() as ctx:
+        sb = ctx.enter_context(tc.tile_pool(name="sb", bufs=1))
+        ps = ctx.enter_context(tc.psum_pool(name="ps", bufs=1))
+
+        def tile(shape, dtype, name):
+            return sb.tile(shape, dtype, name=name, align_bytes=64)
+
+        def deal(copy, dealt, raw, m0, m1):
+            copy(
+                dealt[:, :, m0:m1, :].rearrange("p t m j -> p m j t"),
+                raw[:].rearrange("p j (m t) -> p m j t", t=PACK)[:, m0:m1],
+            )
+
+        def weave(ap_vt):
+            return ap_vt.rearrange("p (c i) t -> p c t i", i=4)
+
+        def planes(ap_tv):
+            return ap_tv.rearrange("p t (c i) -> p c t i", i=4)
+
+        offs_sb = tile([P, S // 16], U16, "offs_sb")
+        pos_sb = [tile([P, V // 16], U16, f"pos_sb{d}") for d in range(2)]
+        xw = tile([P, T], I32, "xw")
+        xs = tile([P, T], U8, "xs")
+        nc.vector.memset(xs[:].bitcast(I32), 0)
+        nc.sync.dma_start(offs_sb[:], offs)
+        for q in range(4):
+            nc.scalar.dma_start(
+                xs[32 * q : 32 * q + 4, :].bitcast(I32), x_scales[0, 4 * q : 4 * q + 4, :].bitcast(I32)
+            )
+        nc.sync.dma_start(xw[:], x_words[0].rearrange("p n t -> p (n t)").bitcast(I32))
+        w1_raw = [tile([P, PACK, H // 2], F32, f"w1_raw{u}") for u in range(2)]
+        w1_rows = w1.rearrange("(p j) c -> p j c", j=PACK)
+        for u in range(2):
+            nc.sync.dma_start(w1_raw[u][:], w1_rows[:, :, u * (H // 2) : (u + 1) * (H // 2)])
+        nc.sync.dma_start(pos_sb[0][:], pos1)
+        nc.sync.dma_start(pos_sb[1][:], pos2)
+        e_raw = tile([P, PACK, V], F32, "e_raw")
+        nc.sync.dma_start(e_raw[:], eT.rearrange("(p j) v -> p j v", j=PACK))
+        gate_sb = tile([P, 2, V], F32, "gate_sb")
+        nc.sync.dma_start(gate_sb[:], gate.rearrange("d p v -> p d v"))
+        w3_raw = tile([P, PACK, N], F32, "w3_raw")
+        nc.sync.dma_start(w3_raw[:], w3.rearrange("(p j) c -> p j c", j=PACK))
+        w2_raw = tile([P, PACK, N], F32, "w2_raw")
+        nc.sync.dma_start(w2_raw[:], w2.rearrange("(p j) c -> p j c", j=PACK))
+
+        xq_s = tile([P, S], U8, "xq_s")
+        xq_w = tile([P, S], U32, "xq_w")
+        nc.vector.tensor_copy(xq_s[:], xs[:].indirect(offs_sb[:]))
+        nc.vector.tensor_copy(xq_w[:], xw[:].bitcast(U32).indirect(offs_sb[:]))
+
+        w1_bf = [tile([P, PACK, P // 2, PACK], BF16, f"w1_bf{u}") for u in range(2)]
+        w1_w = [tile([P, P], U32, f"w1_w{t}") for t in range(PACK)]
+        w1_s = [tile([P, P], U8, f"w1_s{t}") for t in range(PACK)]
+        deal(nc.scalar.copy, w1_bf[0], w1_raw[0], 0, P // 2)
+        deal(nc.scalar.copy, w1_bf[1], w1_raw[1], W1_VECTOR_M, P // 2)
+        deal(nc.vector.tensor_copy, w1_bf[1], w1_raw[1], 0, W1_VECTOR_M)
+        for u in range(2):
+            for t in range(PACK):
+                cols = slice(u * (P // 2), (u + 1) * (P // 2))
+                nc.vector.quantize_mx(
+                    out=w1_w[t][:, cols].bitcast(FP8X4),
+                    scales=w1_s[t][:, cols],
+                    in_=w1_bf[u][:, t].rearrange("p m j -> p (m j)"),
+                )
+
+        h = [tile([P, S], F32, f"h{t}") for t in range(PACK)]
+        for t in range(PACK):
+            acc = ps.tile([P, S], F32, name=f"acc_h{t}", tag=f"bank{t}")
+            nc.tensor.matmul_mx(
+                out=acc[:],
+                lhsT=w1_w[t][:].bitcast(FP8X4),
+                lhsT_scale=w1_s[t][:],
+                rhs=xq_w[:].bitcast(FP8X4),
+                rhs_scale=xq_s[:],
+                start=True,
+                stop=True,
+            )
+            nc.scalar.activation(h[t][:], acc[:], GELU)
+
+        e_bf = tile([P, V, PACK], BF16, "e_bf")
+        e_w = tile([P, V], U32, "e_w")
+        e_s = tile([P, V], U8, "e_s")
+        nc.vector.tensor_copy(weave(e_bf[:]), planes(e_raw[:]))
+        nc.vector.quantize_mx(
+            out=e_w[:].bitcast(FP8X4), scales=e_s[:], in_=e_bf[:].rearrange("p v j -> p (v j)")
+        )
+
+        terms = [tile([P, PACK, V], F32, f"term{d}") for d in range(2)]
+        for t in range(PACK):
+            for d in range(2):
+                nc.vector.tensor_tensor(
+                    terms[d][:, t, :], h[t][:].indirect(pos_sb[d][:]), gate_sb[:, d, :], MULT
+                )
+
+        w3_bf = tile([P, PACK, P, PACK], BF16, "w3_bf")
+        w3_w = tile([P, N], U32, "w3_w")
+        w3_s = tile([P, N], U8, "w3_s")
+        deal(nc.scalar.copy, w3_bf, w3_raw, 0, P)
+        nc.vector.quantize_mx(
+            out=w3_w[:].bitcast(FP8X4), scales=w3_s[:], in_=w3_bf[:].rearrange("p t m j -> p (t m j)")
+        )
+        w2_bf = tile([P, PACK, P, PACK], BF16, "w2_bf")
+        w2_w = tile([P, N], U32, "w2_w")
+        w2_s = tile([P, N], U8, "w2_s")
+        deal(nc.scalar.copy, w2_bf, w2_raw, W2_VECTOR_M, P)
+        deal(nc.vector.tensor_copy, w2_bf, w2_raw, 0, W2_VECTOR_M)
+
+        accs = []
+        for u in range(2):
+            vs = slice(u * HALF_V, (u + 1) * HALF_V)
+            for t in range(PACK):
+                acc = ps.tile([P, HALF_V], F32, name=f"acc_y{u}{t}", tag=f"bank{PACK * (1 - u) + t}")
+                accs.append(acc)
+                nc.tensor.matmul_mx(
+                    out=acc[:],
+                    lhsT=w3_w[:, t * P : (t + 1) * P].bitcast(FP8X4),
+                    lhsT_scale=w3_s[:, t * P : (t + 1) * P],
+                    rhs=e_w[:, vs].bitcast(FP8X4),
+                    rhs_scale=e_s[:, vs],
+                    start=True,
+                    stop=False,
+                )
+
+        z_bf = [tile([P, HALF_V, PACK], BF16, f"z_bf{u}") for u in range(2)]
+        z_w = [tile([P, HALF_V], U32, f"z_w{u}") for u in range(2)]
+        z_s = [tile([P, HALF_V], U8, f"z_s{u}") for u in range(2)]
+        for u in range(2):
+            vs = slice(u * HALF_V, (u + 1) * HALF_V)
+            nc.vector.tensor_tensor(
+                weave(z_bf[u][:]), planes(terms[0][:, :, vs]), planes(terms[1][:, :, vs]), ADD
+            )
+        nc.vector.quantize_mx(
+            out=w2_w[:].bitcast(FP8X4), scales=w2_s[:], in_=w2_bf[:].rearrange("p t m j -> p (t m j)")
+        )
+        for u in range(2):
+            nc.vector.quantize_mx(
+                out=z_w[u][:].bitcast(FP8X4), scales=z_s[u][:], in_=z_bf[u][:].rearrange("p v t -> p (v t)")
+            )
+
+        y = [tile([P, PACK, HALF_V], F32, f"y{u}") for u in range(2)]
+        y_bf = [tile([P, HALF_V, PACK], BF16, f"y_bf{u}") for u in range(2)]
+        y_w = tile([P, V], U32, "y_w")
+        y_s = tile([P, V], U8, "y_s")
+        out_rows = out_0.rearrange("(p t) v -> p t v", t=PACK)
+        out_words = out_1[0].rearrange("p v t -> p (v t)").bitcast(I32)
+        for u in range(2):
+            vs = slice(u * HALF_V, (u + 1) * HALF_V)
+            for t in range(PACK):
+                acc = accs[PACK * u + t]
+                nc.tensor.matmul_mx(
+                    out=acc[:],
+                    lhsT=w2_w[:, t * P : (t + 1) * P].bitcast(FP8X4),
+                    lhsT_scale=w2_s[:, t * P : (t + 1) * P],
+                    rhs=z_w[u][:].bitcast(FP8X4),
+                    rhs_scale=z_s[u][:],
+                    start=False,
+                    stop=True,
+                )
+                nc.scalar.activation(y[u][:, t, :], acc[:], GELU)
+            nc.sync.dma_start(out_rows[:, :, vs], y[u][:])
+            nc.vector.tensor_copy(weave(y_bf[u][:]), planes(y[u][:]))
+            nc.vector.quantize_mx(
+                out=y_w[:, vs].bitcast(FP8X4), scales=y_s[:, vs], in_=y_bf[u][:].rearrange("p v t -> p (v t)")
+            )
+        nc.sync.dma_start(out_words, y_w[:].bitcast(I32))
+        for q in range(4):
+            queue = nc.scalar if q % 2 == 0 else nc.sync
+            queue.dma_start(
+                out_2[0, 4 * q : 4 * q + 4, :].bitcast(I32), y_s[32 * q : 32 * q + 4, :].bitcast(I32)
+            )

@@ -19,8 +19,6 @@ ADD = mybir.AluOpType.add
 P = 128
 PACK = 4
 HALF_V = V // 2
-W1_VECTOR_M = 40
-W2_VECTOR_M = 32
 
 
 def tile_picked_zfp_gelu_po_kernel(
@@ -31,13 +29,13 @@ def tile_picked_zfp_gelu_po_kernel(
         sb = ctx.enter_context(tc.tile_pool(name="sb", bufs=1))
         ps = ctx.enter_context(tc.psum_pool(name="ps", bufs=1))
 
-        def tile(shape, dtype, name):
-            return sb.tile(shape, dtype, name=name, align_bytes=64)
+        def tile(shape, dtype, name, tag=None):
+            return sb.tile(shape, dtype, name=name, tag=tag or name, align_bytes=64)
 
-        def deal(copy, dealt, raw, m0, m1):
+        def deal(copy, dealt, raw, pair):
             copy(
-                dealt[:, :, m0:m1, :].rearrange("p t m j -> p m j t"),
-                raw[:].rearrange("p j (m t) -> p m j t", t=PACK)[:, m0:m1],
+                dealt[:].rearrange("p t m j -> p m j t"),
+                raw[:].rearrange("p j (m t) -> p m j t", t=PACK)[:, :, :, 2 * pair : 2 * pair + 2],
             )
 
         def weave(ap_vt):
@@ -52,11 +50,14 @@ def tile_picked_zfp_gelu_po_kernel(
         xs = tile([P, T], U8, "xs")
         nc.vector.memset(xs[:].bitcast(I32), 0)
         nc.sync.dma_start(offs_sb[:], offs)
+        warm = tile([P, 2], F32, "warm")
+        nc.vector.memset(warm[:, 0:1], 0.0)
+        nc.scalar.activation(warm[:, 1:2], warm[:, 0:1], GELU)
+        nc.sync.dma_start(xw[:], x_words[0].rearrange("p n t -> p (n t)").bitcast(I32))
         for q in range(4):
-            nc.scalar.dma_start(
+            nc.sync.dma_start(
                 xs[32 * q : 32 * q + 4, :].bitcast(I32), x_scales[0, 4 * q : 4 * q + 4, :].bitcast(I32)
             )
-        nc.sync.dma_start(xw[:], x_words[0].rearrange("p n t -> p (n t)").bitcast(I32))
         w1_raw = [tile([P, PACK, H // 2], F32, f"w1_raw{u}") for u in range(2)]
         w1_rows = w1.rearrange("(p j) c -> p j c", j=PACK)
         for u in range(2):
@@ -74,39 +75,42 @@ def tile_picked_zfp_gelu_po_kernel(
 
         xq_s = tile([P, S], U8, "xq_s")
         xq_w = tile([P, S], U32, "xq_w")
-        nc.vector.tensor_copy(xq_s[:], xs[:].indirect(offs_sb[:]))
         nc.vector.tensor_copy(xq_w[:], xw[:].bitcast(U32).indirect(offs_sb[:]))
+        nc.vector.tensor_copy(xq_s[:], xs[:].indirect(offs_sb[:]))
 
-        w1_bf = [tile([P, PACK, P // 2, PACK], BF16, f"w1_bf{u}") for u in range(2)]
+        w1_bf = [[tile([P, 2, P // 2, PACK], BF16, f"w1_bf{u}{pair}") for pair in range(2)] for u in range(2)]
         w1_w = [tile([P, P], U32, f"w1_w{t}") for t in range(PACK)]
         w1_s = [tile([P, P], U8, f"w1_s{t}") for t in range(PACK)]
-        deal(nc.scalar.copy, w1_bf[0], w1_raw[0], 0, P // 2)
-        deal(nc.scalar.copy, w1_bf[1], w1_raw[1], W1_VECTOR_M, P // 2)
-        deal(nc.vector.tensor_copy, w1_bf[1], w1_raw[1], 0, W1_VECTOR_M)
+        deal(nc.scalar.copy, w1_bf[0][0], w1_raw[0], 0)
+        deal(nc.scalar.copy, w1_bf[0][1], w1_raw[0], 1)
+        deal(nc.vector.tensor_copy, w1_bf[1][0], w1_raw[1], 0)
+        deal(nc.scalar.copy, w1_bf[1][1], w1_raw[1], 1)
         for u in range(2):
             for t in range(PACK):
                 cols = slice(u * (P // 2), (u + 1) * (P // 2))
                 nc.vector.quantize_mx(
                     out=w1_w[t][:, cols].bitcast(FP8X4),
                     scales=w1_s[t][:, cols],
-                    in_=w1_bf[u][:, t].rearrange("p m j -> p (m j)"),
+                    in_=w1_bf[u][t // 2][:, t % 2].rearrange("p m j -> p (m j)"),
                 )
 
         h = [tile([P, S], F32, f"h{t}") for t in range(PACK)]
         for t in range(PACK):
-            acc = ps.tile([P, S], F32, name=f"acc_h{t}", tag=f"bank{t}")
-            nc.tensor.matmul_mx(
-                out=acc[:],
-                lhsT=w1_w[t][:].bitcast(FP8X4),
-                lhsT_scale=w1_s[t][:],
-                rhs=xq_w[:].bitcast(FP8X4),
-                rhs_scale=xq_s[:],
-                start=True,
-                stop=True,
-            )
-            nc.scalar.activation(h[t][:], acc[:], GELU)
+            for u in range(2):
+                js = slice(u * (S // 2), (u + 1) * (S // 2))
+                acc = ps.tile([P, S // 2], F32, name=f"acc_h{t}{u}", tag=f"bank{2 * t + u}")
+                nc.tensor.matmul_mx(
+                    out=acc[:],
+                    lhsT=w1_w[t][:].bitcast(FP8X4),
+                    lhsT_scale=w1_s[t][:],
+                    rhs=xq_w[:, js].bitcast(FP8X4),
+                    rhs_scale=xq_s[:, js],
+                    start=True,
+                    stop=True,
+                )
+                nc.scalar.activation(h[t][:, js], acc[:], GELU)
 
-        e_bf = tile([P, V, PACK], BF16, "e_bf")
+        e_bf = tile([P, V, PACK], BF16, "e_bf", "w1_bf11")
         e_w = tile([P, V], U32, "e_w")
         e_s = tile([P, V], U8, "e_s")
         nc.vector.tensor_copy(weave(e_bf[:]), planes(e_raw[:]))
@@ -121,24 +125,33 @@ def tile_picked_zfp_gelu_po_kernel(
                     terms[d][:, t, :], h[t][:].indirect(pos_sb[d][:]), gate_sb[:, d, :], MULT
                 )
 
-        w3_bf = tile([P, PACK, P, PACK], BF16, "w3_bf")
+        w3_bf = [tile([P, 2, P, PACK], BF16, f"w3_bf{pair}", ["w1_w3", None][pair]) for pair in range(2)]
+        w2_bf = [tile([P, 2, P, PACK], BF16, f"w2_bf{pair}") for pair in range(2)]
         w3_w = tile([P, N], U32, "w3_w")
         w3_s = tile([P, N], U8, "w3_s")
-        deal(nc.scalar.copy, w3_bf, w3_raw, 0, P)
-        nc.vector.quantize_mx(
-            out=w3_w[:].bitcast(FP8X4), scales=w3_s[:], in_=w3_bf[:].rearrange("p t m j -> p (t m j)")
-        )
-        w2_bf = tile([P, PACK, P, PACK], BF16, "w2_bf")
         w2_w = tile([P, N], U32, "w2_w")
         w2_s = tile([P, N], U8, "w2_s")
-        deal(nc.scalar.copy, w2_bf, w2_raw, W2_VECTOR_M, P)
-        deal(nc.vector.tensor_copy, w2_bf, w2_raw, 0, W2_VECTOR_M)
+
+        def quantize_pair(words, scales, dealt, pair):
+            cols = slice(2 * P * pair, 2 * P * (pair + 1))
+            nc.vector.quantize_mx(
+                out=words[:, cols].bitcast(FP8X4),
+                scales=scales[:, cols],
+                in_=dealt[pair][:].rearrange("p t m j -> p (t m j)"),
+            )
+
+        for pair in range(2):
+            deal(nc.scalar.copy, w3_bf[pair], w3_raw, pair)
+        for pair in range(2):
+            deal(nc.scalar.copy, w2_bf[pair], w2_raw, pair)
+        for pair in range(2):
+            quantize_pair(w3_w, w3_s, w3_bf, pair)
 
         accs = []
         for u in range(2):
             vs = slice(u * HALF_V, (u + 1) * HALF_V)
             for t in range(PACK):
-                acc = ps.tile([P, HALF_V], F32, name=f"acc_y{u}{t}", tag=f"bank{PACK * (1 - u) + t}")
+                acc = ps.tile([P, HALF_V], F32, name=f"acc_y{u}{t}", tag=f"bank{PACK * u + t}")
                 accs.append(acc)
                 nc.tensor.matmul_mx(
                     out=acc[:],
@@ -150,18 +163,15 @@ def tile_picked_zfp_gelu_po_kernel(
                     stop=False,
                 )
 
-        z_bf = [tile([P, HALF_V, PACK], BF16, f"z_bf{u}") for u in range(2)]
-        z_w = [tile([P, HALF_V], U32, f"z_w{u}") for u in range(2)]
+        z_bf = [tile([P, HALF_V, PACK], BF16, f"z_bf{u}", ["w3_bf1", "w1_w3"][u]) for u in range(2)]
+        z_w = [tile([P, HALF_V], U32, f"z_w{u}", f"w2_bf{u}") for u in range(2)]
         z_s = [tile([P, HALF_V], U8, f"z_s{u}") for u in range(2)]
         for u in range(2):
             vs = slice(u * HALF_V, (u + 1) * HALF_V)
             nc.vector.tensor_tensor(
                 weave(z_bf[u][:]), planes(terms[0][:, :, vs]), planes(terms[1][:, :, vs]), ADD
             )
-        nc.vector.quantize_mx(
-            out=w2_w[:].bitcast(FP8X4), scales=w2_s[:], in_=w2_bf[:].rearrange("p t m j -> p (t m j)")
-        )
-        for u in range(2):
+            quantize_pair(w2_w, w2_s, w2_bf, u)
             nc.vector.quantize_mx(
                 out=z_w[u][:].bitcast(FP8X4), scales=z_s[u][:], in_=z_bf[u][:].rearrange("p v t -> p (v t)")
             )
@@ -191,7 +201,7 @@ def tile_picked_zfp_gelu_po_kernel(
             nc.vector.quantize_mx(
                 out=y_w[:, vs].bitcast(FP8X4), scales=y_s[:, vs], in_=y_bf[u][:].rearrange("p v t -> p (v t)")
             )
-        nc.sync.dma_start(out_words, y_w[:].bitcast(I32))
+            nc.sync.dma_start(out_words[:, vs], y_w[:, vs].bitcast(I32))
         for q in range(4):
             queue = nc.scalar if q % 2 == 0 else nc.sync
             queue.dma_start(

@@ -19,6 +19,7 @@ ADD = mybir.AluOpType.add
 P = 128
 PACK = 4
 HALF_V = V // 2
+QUARTER_V = V // 4
 
 
 def tile_picked_zfp_gelu_po_kernel(
@@ -49,11 +50,11 @@ def tile_picked_zfp_gelu_po_kernel(
         xw = tile([P, T], I32, "xw")
         xs = tile([P, T], U8, "xs")
         nc.vector.memset(xs[:].bitcast(I32), 0)
-        nc.sync.dma_start(offs_sb[:], offs)
         warm = tile([P, 2], F32, "warm")
         nc.vector.memset(warm[:, 0:1], 0.0)
         nc.scalar.activation(warm[:, 1:2], warm[:, 0:1], GELU)
         nc.sync.dma_start(xw[:], x_words[0].rearrange("p n t -> p (n t)").bitcast(I32))
+        nc.sync.dma_start(offs_sb[:], offs)
         for q in range(4):
             nc.sync.dma_start(
                 xs[32 * q : 32 * q + 4, :].bitcast(I32), x_scales[0, 4 * q : 4 * q + 4, :].bitcast(I32)
@@ -62,12 +63,12 @@ def tile_picked_zfp_gelu_po_kernel(
         w1_rows = w1.rearrange("(p j) c -> p j c", j=PACK)
         for u in range(2):
             nc.sync.dma_start(w1_raw[u][:], w1_rows[:, :, u * (H // 2) : (u + 1) * (H // 2)])
-        nc.sync.dma_start(pos_sb[0][:], pos1)
-        nc.sync.dma_start(pos_sb[1][:], pos2)
         e_raw = tile([P, PACK, V], F32, "e_raw")
         nc.sync.dma_start(e_raw[:], eT.rearrange("(p j) v -> p j v", j=PACK))
         gate_sb = tile([P, 2, V], F32, "gate_sb")
         nc.sync.dma_start(gate_sb[:], gate.rearrange("d p v -> p d v"))
+        nc.sync.dma_start(pos_sb[0][:], pos1)
+        nc.sync.dma_start(pos_sb[1][:], pos2)
         w3_raw = tile([P, PACK, N], F32, "w3_raw")
         nc.sync.dma_start(w3_raw[:], w3.rearrange("(p j) c -> p j c", j=PACK))
         w2_raw = tile([P, PACK, N], F32, "w2_raw")
@@ -85,14 +86,15 @@ def tile_picked_zfp_gelu_po_kernel(
         deal(nc.scalar.copy, w1_bf[0][1], w1_raw[0], 1)
         deal(nc.vector.tensor_copy, w1_bf[1][0], w1_raw[1], 0)
         deal(nc.scalar.copy, w1_bf[1][1], w1_raw[1], 1)
-        for u in range(2):
-            for t in range(PACK):
-                cols = slice(u * (P // 2), (u + 1) * (P // 2))
-                nc.vector.quantize_mx(
-                    out=w1_w[t][:, cols].bitcast(FP8X4),
-                    scales=w1_s[t][:, cols],
-                    in_=w1_bf[u][t // 2][:, t % 2].rearrange("p m j -> p (m j)"),
-                )
+        for pair in range(2):
+            for u in range(2):
+                for t in (2 * pair, 2 * pair + 1):
+                    cols = slice(u * (P // 2), (u + 1) * (P // 2))
+                    nc.vector.quantize_mx(
+                        out=w1_w[t][:, cols].bitcast(FP8X4),
+                        scales=w1_s[t][:, cols],
+                        in_=w1_bf[u][pair][:, t % 2].rearrange("p m j -> p (m j)"),
+                    )
 
         h = [tile([P, S], F32, f"h{t}") for t in range(PACK)]
         for t in range(PACK):
@@ -110,13 +112,16 @@ def tile_picked_zfp_gelu_po_kernel(
                 )
                 nc.scalar.activation(h[t][:, js], acc[:], GELU)
 
-        e_bf = tile([P, V, PACK], BF16, "e_bf", "w1_bf11")
+        e_bf = [tile([P, HALF_V, PACK], BF16, f"e_bf{u}", f"w1_bf{u}1") for u in range(2)]
         e_w = tile([P, V], U32, "e_w")
         e_s = tile([P, V], U8, "e_s")
-        nc.vector.tensor_copy(weave(e_bf[:]), planes(e_raw[:]))
-        nc.vector.quantize_mx(
-            out=e_w[:].bitcast(FP8X4), scales=e_s[:], in_=e_bf[:].rearrange("p v j -> p (v j)")
-        )
+        for u in range(2):
+            nc.vector.tensor_copy(weave(e_bf[u][:]), planes(e_raw[:, :, u * HALF_V : (u + 1) * HALF_V]))
+        for u in range(2):
+            vs = slice(u * HALF_V, (u + 1) * HALF_V)
+            nc.vector.quantize_mx(
+                out=e_w[:, vs].bitcast(FP8X4), scales=e_s[:, vs], in_=e_bf[u][:].rearrange("p v j -> p (v j)")
+            )
 
         terms = [tile([P, PACK, V], F32, f"term{d}") for d in range(2)]
         for t in range(PACK):
@@ -177,7 +182,7 @@ def tile_picked_zfp_gelu_po_kernel(
             )
 
         y = [tile([P, PACK, HALF_V], F32, f"y{u}") for u in range(2)]
-        y_bf = [tile([P, HALF_V, PACK], BF16, f"y_bf{u}") for u in range(2)]
+        y_bf = [[tile([P, QUARTER_V, PACK], BF16, f"y_bf{u}{c}") for c in range(2)] for u in range(2)]
         y_w = tile([P, V], U32, "y_w")
         y_s = tile([P, V], U8, "y_s")
         out_rows = out_0.rearrange("(p t) v -> p t v", t=PACK)
@@ -197,10 +202,16 @@ def tile_picked_zfp_gelu_po_kernel(
                 )
                 nc.scalar.activation(y[u][:, t, :], acc[:], GELU)
             nc.sync.dma_start(out_rows[:, :, vs], y[u][:])
-            nc.vector.tensor_copy(weave(y_bf[u][:]), planes(y[u][:]))
-            nc.vector.quantize_mx(
-                out=y_w[:, vs].bitcast(FP8X4), scales=y_s[:, vs], in_=y_bf[u][:].rearrange("p v t -> p (v t)")
-            )
+            for c in range(2):
+                copy = nc.scalar.copy if (u, c) == (1, 0) else nc.vector.tensor_copy
+                copy(weave(y_bf[u][c][:]), planes(y[u][:, :, c * QUARTER_V : (c + 1) * QUARTER_V]))
+            for c in range(2):
+                cols = slice((2 * u + c) * QUARTER_V, (2 * u + c + 1) * QUARTER_V)
+                nc.vector.quantize_mx(
+                    out=y_w[:, cols].bitcast(FP8X4),
+                    scales=y_s[:, cols],
+                    in_=y_bf[u][c][:].rearrange("p v t -> p (v t)"),
+                )
             nc.sync.dma_start(out_words[:, vs], y_w[:, vs].bitcast(I32))
         for q in range(4):
             queue = nc.scalar if q % 2 == 0 else nc.sync

@@ -20,6 +20,7 @@ P = 128
 PACK = 4
 HALF_V = V // 2
 QUARTER_V = V // 4
+W1_VECTOR_M = 40
 
 
 def tile_picked_zfp_gelu_po_kernel(
@@ -33,10 +34,10 @@ def tile_picked_zfp_gelu_po_kernel(
         def tile(shape, dtype, name, tag=None):
             return sb.tile(shape, dtype, name=name, tag=tag or name, align_bytes=64)
 
-        def deal(copy, dealt, raw, pair):
+        def deal(copy, dealt, raw, m0, m1):
             copy(
-                dealt[:].rearrange("p t m j -> p m j t"),
-                raw[:].rearrange("p j (m t) -> p m j t", t=PACK)[:, :, :, 2 * pair : 2 * pair + 2],
+                dealt[:, :, m0:m1, :].rearrange("p t m j -> p m j t"),
+                raw[:].rearrange("p j (m t) -> p m j t", t=PACK)[:, m0:m1],
             )
 
         def weave(ap_vt):
@@ -79,13 +80,12 @@ def tile_picked_zfp_gelu_po_kernel(
         nc.vector.tensor_copy(xq_w[:], xw[:].bitcast(U32).indirect(offs_sb[:]))
         nc.vector.tensor_copy(xq_s[:], xs[:].indirect(offs_sb[:]))
 
-        w1_bf = [[tile([P, 2, P // 2, PACK], BF16, f"w1_bf{u}{pair}") for pair in range(2)] for u in range(2)]
+        w1_bf = [tile([P, PACK, P // 2, PACK], BF16, f"w1_bf{u}") for u in range(2)]
         w1_w = [tile([P, P], U32, f"w1_w{t}") for t in range(PACK)]
         w1_s = [tile([P, P], U8, f"w1_s{t}") for t in range(PACK)]
-        deal(nc.scalar.copy, w1_bf[0][0], w1_raw[0], 0)
-        deal(nc.scalar.copy, w1_bf[0][1], w1_raw[0], 1)
-        deal(nc.vector.tensor_copy, w1_bf[1][0], w1_raw[1], 0)
-        deal(nc.scalar.copy, w1_bf[1][1], w1_raw[1], 1)
+        deal(nc.scalar.copy, w1_bf[0], w1_raw[0], 0, P // 2)
+        deal(nc.vector.tensor_copy, w1_bf[1], w1_raw[1], 0, W1_VECTOR_M)
+        deal(nc.scalar.copy, w1_bf[1], w1_raw[1], W1_VECTOR_M, P // 2)
         for pair in range(2):
             for u in range(2):
                 for t in (2 * pair, 2 * pair + 1):
@@ -93,7 +93,7 @@ def tile_picked_zfp_gelu_po_kernel(
                     nc.vector.quantize_mx(
                         out=w1_w[t][:, cols].bitcast(FP8X4),
                         scales=w1_s[t][:, cols],
-                        in_=w1_bf[u][pair][:, t % 2].rearrange("p m j -> p (m j)"),
+                        in_=w1_bf[u][:, t].rearrange("p m j -> p (m j)"),
                     )
 
         h = [tile([P, S], F32, f"h{t}") for t in range(PACK)]
@@ -112,7 +112,7 @@ def tile_picked_zfp_gelu_po_kernel(
                 )
                 nc.scalar.activation(h[t][:, js], acc[:], GELU)
 
-        e_bf = [tile([P, HALF_V, PACK], BF16, f"e_bf{u}", f"w1_bf{u}1") for u in range(2)]
+        e_bf = [tile([P, HALF_V, PACK], BF16, f"e_bf{u}", f"w1_bf{u}") for u in range(2)]
         e_w = tile([P, V], U32, "e_w")
         e_s = tile([P, V], U8, "e_s")
         for u in range(2):
@@ -130,27 +130,17 @@ def tile_picked_zfp_gelu_po_kernel(
                     terms[d][:, t, :], h[t][:].indirect(pos_sb[d][:]), gate_sb[:, d, :], MULT
                 )
 
-        w3_bf = [tile([P, 2, P, PACK], BF16, f"w3_bf{pair}", ["w1_w3", None][pair]) for pair in range(2)]
-        w2_bf = [tile([P, 2, P, PACK], BF16, f"w2_bf{pair}") for pair in range(2)]
+        w3_bf = tile([P, PACK, P, PACK], BF16, "w3_bf", "w1_w3")
+        w2_bf = tile([P, PACK, P, PACK], BF16, "w2_bf")
         w3_w = tile([P, N], U32, "w3_w")
         w3_s = tile([P, N], U8, "w3_s")
         w2_w = tile([P, N], U32, "w2_w")
         w2_s = tile([P, N], U8, "w2_s")
-
-        def quantize_pair(words, scales, dealt, pair):
-            cols = slice(2 * P * pair, 2 * P * (pair + 1))
-            nc.vector.quantize_mx(
-                out=words[:, cols].bitcast(FP8X4),
-                scales=scales[:, cols],
-                in_=dealt[pair][:].rearrange("p t m j -> p (t m j)"),
-            )
-
-        for pair in range(2):
-            deal(nc.scalar.copy, w3_bf[pair], w3_raw, pair)
-        for pair in range(2):
-            deal(nc.scalar.copy, w2_bf[pair], w2_raw, pair)
-        for pair in range(2):
-            quantize_pair(w3_w, w3_s, w3_bf, pair)
+        deal(nc.scalar.copy, w3_bf, w3_raw, 0, P)
+        deal(nc.scalar.copy, w2_bf, w2_raw, 0, P)
+        nc.vector.quantize_mx(
+            out=w3_w[:].bitcast(FP8X4), scales=w3_s[:], in_=w3_bf[:].rearrange("p t m j -> p (t m j)")
+        )
 
         accs = []
         for u in range(2):
@@ -168,17 +158,24 @@ def tile_picked_zfp_gelu_po_kernel(
                     stop=False,
                 )
 
-        z_bf = [tile([P, HALF_V, PACK], BF16, f"z_bf{u}", ["w3_bf1", "w1_w3"][u]) for u in range(2)]
-        z_w = [tile([P, HALF_V], U32, f"z_w{u}", f"w2_bf{u}") for u in range(2)]
-        z_s = [tile([P, HALF_V], U8, f"z_s{u}") for u in range(2)]
+        z_bf = tile([P, V, PACK], BF16, "z_bf", "w1_w3")
+        z_w = tile([P, V], U32, "z_w")
+        z_s = tile([P, V], U8, "z_s", "w2_raw")
         for u in range(2):
             vs = slice(u * HALF_V, (u + 1) * HALF_V)
             nc.vector.tensor_tensor(
-                weave(z_bf[u][:]), planes(terms[0][:, :, vs]), planes(terms[1][:, :, vs]), ADD
+                weave(z_bf[:, vs, :]), planes(terms[0][:, :, vs]), planes(terms[1][:, :, vs]), ADD
             )
-            quantize_pair(w2_w, w2_s, w2_bf, u)
+        for u in range(2):
+            vs = slice(u * HALF_V, (u + 1) * HALF_V)
+            ms = slice(u * (N // 2), (u + 1) * (N // 2))
             nc.vector.quantize_mx(
-                out=z_w[u][:].bitcast(FP8X4), scales=z_s[u][:], in_=z_bf[u][:].rearrange("p v t -> p (v t)")
+                out=w2_w[:, ms].bitcast(FP8X4),
+                scales=w2_s[:, ms],
+                in_=w2_bf[:, 2 * u : 2 * u + 2].rearrange("p t m j -> p (t m j)"),
+            )
+            nc.vector.quantize_mx(
+                out=z_w[:, vs].bitcast(FP8X4), scales=z_s[:, vs], in_=z_bf[:, vs, :].rearrange("p v t -> p (v t)")
             )
 
         y = [tile([P, PACK, HALF_V], F32, f"y{u}") for u in range(2)]
@@ -195,8 +192,8 @@ def tile_picked_zfp_gelu_po_kernel(
                     out=acc[:],
                     lhsT=w2_w[:, t * P : (t + 1) * P].bitcast(FP8X4),
                     lhsT_scale=w2_s[:, t * P : (t + 1) * P],
-                    rhs=z_w[u][:].bitcast(FP8X4),
-                    rhs_scale=z_s[u][:],
+                    rhs=z_w[:, vs].bitcast(FP8X4),
+                    rhs_scale=z_s[:, vs],
                     start=False,
                     stop=True,
                 )

@@ -158,7 +158,7 @@ def tile_picked_zfp_gelu_po_kernel(
                     stop=False,
                 )
 
-        z_bf = tile([P, V, PACK], BF16, "z_bf", "w1_w3")
+        z_bf = tile([P, V, PACK], BF16, "z_bf", "w3_raw")
         z_w = tile([P, V], U32, "z_w")
         z_s = tile([P, V], U8, "z_s", "w2_raw")
         for u in range(2):
@@ -198,7 +198,10 @@ def tile_picked_zfp_gelu_po_kernel(
                     stop=True,
                 )
                 nc.scalar.activation(y[u][:, t, :], acc[:], GELU)
-            nc.sync.dma_start(out_rows[:, :, vs], y[u][:])
+                if u == 1 and t % 2 == 1:
+                    nc.sync.dma_start(out_rows[:, t - 1 : t + 1, vs], y[u][:, t - 1 : t + 1])
+            if u == 0:
+                nc.sync.dma_start(out_rows[:, :, vs], y[u][:])
             for c in range(2):
                 copy = nc.scalar.copy if (u, c) == (1, 0) else nc.vector.tensor_copy
                 copy(weave(y_bf[u][c][:]), planes(y[u][:, :, c * QUARTER_V : (c + 1) * QUARTER_V]))
@@ -209,7 +212,7 @@ def tile_picked_zfp_gelu_po_kernel(
                     scales=y_s[:, cols],
                     in_=y_bf[u][c][:].rearrange("p v t -> p (v t)"),
                 )
-            nc.sync.dma_start(out_words[:, vs], y_w[:, vs].bitcast(I32))
+        nc.sync.dma_start(out_words, y_w[:].bitcast(I32))
         for q in range(4):
             queue = nc.scalar if q % 2 == 0 else nc.sync
             queue.dma_start(

@@ -166,52 +166,57 @@ def tile_picked_zfp_gelu_po_kernel(
             nc.vector.tensor_tensor(
                 weave(z_bf[:, vs, :]), planes(terms[0][:, :, vs]), planes(terms[1][:, :, vs]), ADD
             )
-        for u in range(2):
-            vs = slice(u * HALF_V, (u + 1) * HALF_V)
-            ms = slice(u * (N // 2), (u + 1) * (N // 2))
+
+        def quantise_w2(pair):
+            ms = slice(pair * (N // 2), (pair + 1) * (N // 2))
             nc.vector.quantize_mx(
                 out=w2_w[:, ms].bitcast(FP8X4),
                 scales=w2_s[:, ms],
-                in_=w2_bf[:, 2 * u : 2 * u + 2].rearrange("p t m j -> p (t m j)"),
+                in_=w2_bf[:, 2 * pair : 2 * pair + 2].rearrange("p t m j -> p (t m j)"),
             )
+
+        quantise_w2(0)
+        for u in range(2):
+            vs = slice(u * HALF_V, (u + 1) * HALF_V)
             nc.vector.quantize_mx(
                 out=z_w[:, vs].bitcast(FP8X4), scales=z_s[:, vs], in_=z_bf[:, vs, :].rearrange("p v t -> p (v t)")
             )
+        quantise_w2(1)
 
-        y = [tile([P, PACK, HALF_V], F32, f"y{u}") for u in range(2)]
-        y_bf = [[tile([P, QUARTER_V, PACK], BF16, f"y_bf{u}{c}") for c in range(2)] for u in range(2)]
+        y = tile([P, PACK, V], F32, "y")
+        y_bf = [tile([P, n, PACK], BF16, f"y_bf{c}") for c, n in enumerate((HALF_V, QUARTER_V, QUARTER_V))]
         y_w = tile([P, V], U32, "y_w")
         y_s = tile([P, V], U8, "y_s")
         out_rows = out_0.rearrange("(p t) v -> p t v", t=PACK)
         out_words = out_1[0].rearrange("p v t -> p (v t)").bitcast(I32)
-        for u in range(2):
-            vs = slice(u * HALF_V, (u + 1) * HALF_V)
-            for t in range(PACK):
-                acc = accs[PACK * u + t]
-                nc.tensor.matmul_mx(
-                    out=acc[:],
-                    lhsT=w2_w[:, t * P : (t + 1) * P].bitcast(FP8X4),
-                    lhsT_scale=w2_s[:, t * P : (t + 1) * P],
-                    rhs=z_w[:, vs].bitcast(FP8X4),
-                    rhs_scale=z_s[:, vs],
-                    start=False,
-                    stop=True,
-                )
-                nc.scalar.activation(y[u][:, t, :], acc[:], GELU)
-                if u == 1 and t % 2 == 1:
-                    nc.sync.dma_start(out_rows[:, t - 1 : t + 1, vs], y[u][:, t - 1 : t + 1])
-            if u == 0:
-                nc.sync.dma_start(out_rows[:, :, vs], y[u][:])
-            for c in range(2):
-                copy = nc.scalar.copy if (u, c) == (1, 0) else nc.vector.tensor_copy
-                copy(weave(y_bf[u][c][:]), planes(y[u][:, :, c * QUARTER_V : (c + 1) * QUARTER_V]))
-            for c in range(2):
-                cols = slice((2 * u + c) * QUARTER_V, (2 * u + c + 1) * QUARTER_V)
-                nc.vector.quantize_mx(
-                    out=y_w[:, cols].bitcast(FP8X4),
-                    scales=y_s[:, cols],
-                    in_=y_bf[u][c][:].rearrange("p v t -> p (v t)"),
-                )
+        for pair in range(2):
+            ts = slice(2 * pair, 2 * pair + 2)
+            for u in range(2):
+                vs = slice(u * HALF_V, (u + 1) * HALF_V)
+                for t in (2 * pair, 2 * pair + 1):
+                    acc = accs[PACK * u + t]
+                    nc.tensor.matmul_mx(
+                        out=acc[:],
+                        lhsT=w2_w[:, t * P : (t + 1) * P].bitcast(FP8X4),
+                        lhsT_scale=w2_s[:, t * P : (t + 1) * P],
+                        rhs=z_w[:, vs].bitcast(FP8X4),
+                        rhs_scale=z_s[:, vs],
+                        start=False,
+                        stop=True,
+                    )
+                    nc.scalar.activation(y[:, t, vs], acc[:], GELU)
+                if pair == 1:
+                    nc.sync.dma_start(out_rows[:, ts, vs], y[:, ts, vs])
+            if pair == 0:
+                nc.sync.dma_start(out_rows[:, ts, :], y[:, ts, :])
+        pieces = (slice(0, HALF_V), slice(HALF_V, HALF_V + QUARTER_V), slice(HALF_V + QUARTER_V, V))
+        for c, cols in enumerate(pieces):
+            copy = nc.scalar.copy if c == 1 else nc.vector.tensor_copy
+            copy(weave(y_bf[c][:]), planes(y[:, :, cols]))
+        for c, cols in enumerate(pieces):
+            nc.vector.quantize_mx(
+                out=y_w[:, cols].bitcast(FP8X4), scales=y_s[:, cols], in_=y_bf[c][:].rearrange("p v t -> p (v t)")
+            )
         nc.sync.dma_start(out_words, y_w[:].bitcast(I32))
         for q in range(4):
             queue = nc.scalar if q % 2 == 0 else nc.sync

@@ -40,6 +40,12 @@ def tile_picked_zfp_gelu_po_kernel(
                 raw[:].rearrange("p j (m t) -> p m j t", t=PACK)[:, m0:m1],
             )
 
+        def deal_pair(copy, dealt, raw, pair):
+            copy(
+                dealt[:].rearrange("p b m j -> p m j b"),
+                raw[:].rearrange("p j (m a b) -> p a m j b", a=2, b=2)[:, pair],
+            )
+
         def weave(ap_vt):
             return ap_vt.rearrange("p (c i) t -> p c t i", i=4)
 
@@ -131,13 +137,14 @@ def tile_picked_zfp_gelu_po_kernel(
                 )
 
         w3_bf = tile([P, PACK, P, PACK], BF16, "w3_bf", "w1_w3")
-        w2_bf = tile([P, PACK, P, PACK], BF16, "w2_bf")
+        w2_bf = [tile([P, 2, P, PACK], BF16, f"w2_bf{pair}") for pair in range(2)]
         w3_w = tile([P, N], U32, "w3_w")
         w3_s = tile([P, N], U8, "w3_s")
         w2_w = tile([P, N], U32, "w2_w")
         w2_s = tile([P, N], U8, "w2_s")
         deal(nc.scalar.copy, w3_bf, w3_raw, 0, P)
-        deal(nc.scalar.copy, w2_bf, w2_raw, 0, P)
+        for pair in range(2):
+            deal_pair(nc.scalar.copy, w2_bf[pair], w2_raw, pair)
         nc.vector.quantize_mx(
             out=w3_w[:].bitcast(FP8X4), scales=w3_s[:], in_=w3_bf[:].rearrange("p t m j -> p (t m j)")
         )
@@ -160,28 +167,28 @@ def tile_picked_zfp_gelu_po_kernel(
 
         z_bf = tile([P, V, PACK], BF16, "z_bf", "w3_raw")
         z_w = tile([P, V], U32, "z_w")
-        z_s = tile([P, V], U8, "z_s", "w2_raw")
+        z_s = tile([P, V], U8, "z_s")
         for u in range(2):
             vs = slice(u * HALF_V, (u + 1) * HALF_V)
             nc.vector.tensor_tensor(
                 weave(z_bf[:, vs, :]), planes(terms[0][:, :, vs]), planes(terms[1][:, :, vs]), ADD
             )
 
-        def quantise_w2(pair):
-            ms = slice(pair * (N // 2), (pair + 1) * (N // 2))
+        def quantise_w2(t0, t1):
+            ms = slice(t0 * P, t1 * P)
             nc.vector.quantize_mx(
                 out=w2_w[:, ms].bitcast(FP8X4),
                 scales=w2_s[:, ms],
-                in_=w2_bf[:, 2 * pair : 2 * pair + 2].rearrange("p t m j -> p (t m j)"),
+                in_=w2_bf[t0 // 2][:, t0 % 2 : t0 % 2 + t1 - t0].rearrange("p t m j -> p (t m j)"),
             )
 
-        quantise_w2(0)
         for u in range(2):
             vs = slice(u * HALF_V, (u + 1) * HALF_V)
             nc.vector.quantize_mx(
                 out=z_w[:, vs].bitcast(FP8X4), scales=z_s[:, vs], in_=z_bf[:, vs, :].rearrange("p v t -> p (v t)")
             )
-        quantise_w2(1)
+        for t0, t1 in ((0, 1), (1, 2), (2, 4)):
+            quantise_w2(t0, t1)
 
         y = tile([P, PACK, V], F32, "y")
         y_bf = [tile([P, n, PACK], BF16, f"y_bf{c}") for c, n in enumerate((HALF_V, QUARTER_V, QUARTER_V))]
@@ -191,9 +198,10 @@ def tile_picked_zfp_gelu_po_kernel(
         out_words = out_1[0].rearrange("p v t -> p (v t)").bitcast(I32)
         for pair in range(2):
             ts = slice(2 * pair, 2 * pair + 2)
-            for u in range(2):
+            order = [(u, t) for t in (0, 1) for u in range(2)] if pair == 0 else [(u, t) for u in range(2) for t in (2, 3)]
+            for u, t in order:
                 vs = slice(u * HALF_V, (u + 1) * HALF_V)
-                for t in (2 * pair, 2 * pair + 1):
+                if True:
                     acc = accs[PACK * u + t]
                     nc.tensor.matmul_mx(
                         out=acc[:],
@@ -205,7 +213,7 @@ def tile_picked_zfp_gelu_po_kernel(
                         stop=True,
                     )
                     nc.scalar.activation(y[:, t, vs], acc[:], GELU)
-                if pair == 1:
+                if t == 3:
                     nc.sync.dma_start(out_rows[:, ts, vs], y[:, ts, vs])
             if pair == 0:
                 nc.sync.dma_start(out_rows[:, ts, :], y[:, ts, :])

@@ -20,7 +20,7 @@ P = 128
 PACK = 4
 HALF_V = V // 2
 QUARTER_V = V // 4
-W1_VECTOR_M = 40
+PIECES = ((0, 256), (256, 384), (384, 512))
 
 
 def tile_picked_zfp_gelu_po_kernel(
@@ -29,6 +29,7 @@ def tile_picked_zfp_gelu_po_kernel(
     nc = tc.nc
     with ExitStack() as ctx:
         sb = ctx.enter_context(tc.tile_pool(name="sb", bufs=1))
+        shared = ctx.enter_context(tc.tile_pool(name="shared", bufs=1))
         ps = ctx.enter_context(tc.psum_pool(name="ps", bufs=1))
 
         def tile(shape, dtype, name, tag=None):
@@ -55,21 +56,21 @@ def tile_picked_zfp_gelu_po_kernel(
         offs_sb = tile([P, S // 16], U16, "offs_sb")
         pos_sb = [tile([P, V // 16], U16, f"pos_sb{d}") for d in range(2)]
         xw = tile([P, T], I32, "xw")
-        xs = tile([P, T], U8, "xs")
+        xs = shared.tile([P, T], U8, name="xs", align_bytes=64, offset=0)
         nc.vector.memset(xs[:].bitcast(I32), 0)
         warm = tile([P, 2], F32, "warm")
         nc.vector.memset(warm[:, 0:1], 0.0)
         nc.scalar.activation(warm[:, 1:2], warm[:, 0:1], GELU)
-        nc.sync.dma_start(xw[:], x_words[0].rearrange("p n t -> p (n t)").bitcast(I32))
+        w1_raw = [tile([P, PACK, H // 2], F32, f"w1_raw{u}") for u in range(2)]
+        w1_rows = w1.rearrange("(p j) c -> p j c", j=PACK)
+        nc.sync.dma_start(w1_raw[0][:], w1_rows[:, :, : H // 2])
         nc.sync.dma_start(offs_sb[:], offs)
         for q in range(4):
             nc.sync.dma_start(
                 xs[32 * q : 32 * q + 4, :].bitcast(I32), x_scales[0, 4 * q : 4 * q + 4, :].bitcast(I32)
             )
-        w1_raw = [tile([P, PACK, H // 2], F32, f"w1_raw{u}") for u in range(2)]
-        w1_rows = w1.rearrange("(p j) c -> p j c", j=PACK)
-        for u in range(2):
-            nc.sync.dma_start(w1_raw[u][:], w1_rows[:, :, u * (H // 2) : (u + 1) * (H // 2)])
+        nc.sync.dma_start(w1_raw[1][:], w1_rows[:, :, H // 2 :])
+        nc.sync.dma_start(xw[:], x_words[0].rearrange("p n t -> p (n t)").bitcast(I32))
         e_raw = tile([P, PACK, V], F32, "e_raw")
         nc.sync.dma_start(e_raw[:], eT.rearrange("(p j) v -> p j v", j=PACK))
         gate_sb = tile([P, 2, V], F32, "gate_sb")
@@ -83,34 +84,46 @@ def tile_picked_zfp_gelu_po_kernel(
 
         xq_s = tile([P, S], U8, "xq_s")
         xq_w = tile([P, S], U32, "xq_w")
-        nc.vector.tensor_copy(xq_w[:], xw[:].bitcast(U32).indirect(offs_sb[:]))
         nc.vector.tensor_copy(xq_s[:], xs[:].indirect(offs_sb[:]))
 
-        w1_bf = [tile([P, PACK, P // 2, PACK], BF16, f"w1_bf{u}") for u in range(2)]
+        w1_bf = [
+            tile([P, PACK, P // 2, PACK], BF16, "w1_bf0"),
+            tile([P, PACK, P // 2, PACK], BF16, "w1_bf1"),
+        ]
         w1_w = [tile([P, P], U32, f"w1_w{t}") for t in range(PACK)]
-        w1_s = [tile([P, P], U8, f"w1_s{t}") for t in range(PACK)]
+        w1_s = shared.tile([P, PACK, P], U8, name="w1_s", align_bytes=64, offset=0)
         deal(nc.scalar.copy, w1_bf[0], w1_raw[0], 0, P // 2)
-        deal(nc.vector.tensor_copy, w1_bf[1], w1_raw[1], 0, W1_VECTOR_M)
-        deal(nc.scalar.copy, w1_bf[1], w1_raw[1], W1_VECTOR_M, P // 2)
         for pair in range(2):
-            for u in range(2):
-                for t in (2 * pair, 2 * pair + 1):
-                    cols = slice(u * (P // 2), (u + 1) * (P // 2))
-                    nc.vector.quantize_mx(
-                        out=w1_w[t][:, cols].bitcast(FP8X4),
-                        scales=w1_s[t][:, cols],
-                        in_=w1_bf[u][:, t].rearrange("p m j -> p (m j)"),
-                    )
+            nc.scalar.copy(
+                w1_bf[1][:, 2 * pair : 2 * pair + 2].rearrange("p b m j -> p m j b"),
+                w1_raw[1][:].rearrange("p j (m a b) -> p a m j b", a=2, b=2)[:, pair],
+            )
+
+        def quantise_w1(u, t):
+            cols = slice(u * (P // 2), (u + 1) * (P // 2))
+            nc.vector.quantize_mx(
+                out=w1_w[t][:, cols].bitcast(FP8X4),
+                scales=w1_s[:, t, cols],
+                in_=w1_bf[u][:, t].rearrange("p m j -> p (m j)"),
+            )
+
+        for t in range(PACK):
+            quantise_w1(0, t)
+        quantise_w1(1, 0)
+        for j0, j1 in PIECES:
+            nc.vector.tensor_copy(xq_w[:, j0:j1], xw[:].bitcast(U32).indirect(offs_sb[:, j0 // 16 : j1 // 16]))
+        for t in range(1, PACK):
+            quantise_w1(1, t)
 
         h = [tile([P, S], F32, f"h{t}") for t in range(PACK)]
         for t in range(PACK):
-            for u in range(2):
-                js = slice(u * (S // 2), (u + 1) * (S // 2))
-                acc = ps.tile([P, S // 2], F32, name=f"acc_h{t}{u}", tag=f"bank{2 * t + u}")
+            for u, (j0, j1) in enumerate(PIECES if t == 0 else ((0, 256), (256, 512))):
+                js = slice(j0, j1)
+                acc = ps.tile([P, j1 - j0], F32, name=f"acc_h{t}{u}", tag=f"bank{(2 * t + u + (t > 0)) % 8}")
                 nc.tensor.matmul_mx(
                     out=acc[:],
                     lhsT=w1_w[t][:].bitcast(FP8X4),
-                    lhsT_scale=w1_s[t][:],
+                    lhsT_scale=w1_s[:, t, :],
                     rhs=xq_w[:, js].bitcast(FP8X4),
                     rhs_scale=xq_s[:, js],
                     start=True,
@@ -118,7 +131,7 @@ def tile_picked_zfp_gelu_po_kernel(
                 )
                 nc.scalar.activation(h[t][:, js], acc[:], GELU)
 
-        e_bf = [tile([P, HALF_V, PACK], BF16, f"e_bf{u}", f"w1_bf{u}") for u in range(2)]
+        e_bf = [tile([P, HALF_V, PACK], BF16, f"e_bf{u}") for u in range(2)]
         e_w = tile([P, V], U32, "e_w")
         e_s = tile([P, V], U8, "e_s")
         for u in range(2):
@@ -213,10 +226,7 @@ def tile_picked_zfp_gelu_po_kernel(
                         stop=True,
                     )
                     nc.scalar.activation(y[:, t, vs], acc[:], GELU)
-                if t == 3:
-                    nc.sync.dma_start(out_rows[:, ts, vs], y[:, ts, vs])
-            if pair == 0:
-                nc.sync.dma_start(out_rows[:, ts, :], y[:, ts, :])
+            nc.sync.dma_start(out_rows[:, ts, :], y[:, ts, :])
         pieces = (slice(0, HALF_V), slice(HALF_V, HALF_V + QUARTER_V), slice(HALF_V + QUARTER_V, V))
         for c, cols in enumerate(pieces):
             copy = nc.scalar.copy if c == 1 else nc.vector.tensor_copy
@@ -225,7 +235,9 @@ def tile_picked_zfp_gelu_po_kernel(
             nc.vector.quantize_mx(
                 out=y_w[:, cols].bitcast(FP8X4), scales=y_s[:, cols], in_=y_bf[c][:].rearrange("p v t -> p (v t)")
             )
-        nc.sync.dma_start(out_words, y_w[:].bitcast(I32))
+            if c != 1:
+                vs = slice(c // 2 * HALF_V, (c // 2 + 1) * HALF_V)
+                nc.sync.dma_start(out_words[:, vs], y_w[:, vs].bitcast(I32))
         for q in range(4):
             queue = nc.scalar if q % 2 == 0 else nc.sync
             queue.dma_start(

@@ -13,6 +13,7 @@ U16 = mybir.dt.uint16
 U8 = mybir.dt.uint8
 FP8X4 = mybir.dt.float8_e4m3fn_x4
 GELU = mybir.ActivationFunctionType.Gelu_apprx_tanh
+COPY = mybir.ActivationFunctionType.Copy
 MULT = mybir.AluOpType.mult
 ADD = mybir.AluOpType.add
 
@@ -20,7 +21,11 @@ P = 128
 PACK = 4
 HALF_V = V // 2
 QUARTER_V = V // 4
-PIECES = ((0, 256), (256, 384), (384, 512))
+QUADRANTS = 4
+BANKS = 8
+WORD_PIECES = ((0, 128), (128, 384), (384, 512))
+ON_SCALAR = (PACK - 1, 1)
+LIST_HALVES = ((0, S // 2), (S // 2, S))
 
 
 def tile_picked_zfp_gelu_po_kernel(
@@ -35,16 +40,16 @@ def tile_picked_zfp_gelu_po_kernel(
         def tile(shape, dtype, name, tag=None):
             return sb.tile(shape, dtype, name=name, tag=tag or name, align_bytes=64)
 
-        def deal(copy, dealt, raw, m0, m1):
-            copy(
-                dealt[:, :, m0:m1, :].rearrange("p t m j -> p m j t"),
-                raw[:].rearrange("p j (m t) -> p m j t", t=PACK)[:, m0:m1],
+        def deal(dealt, raw):
+            nc.scalar.copy(
+                dealt.rearrange("p t m j -> p m j t"),
+                raw.rearrange("p j (m t) -> p m j t", t=PACK),
             )
 
-        def deal_pair(copy, dealt, raw, pair):
-            copy(
-                dealt[:].rearrange("p b m j -> p m j b"),
-                raw[:].rearrange("p j (m a b) -> p a m j b", a=2, b=2)[:, pair],
+        def deal_pair(dealt, raw, pair):
+            nc.scalar.copy(
+                dealt.rearrange("p b m j -> p m j b"),
+                raw.rearrange("p j (m a b) -> p a m j b", a=2, b=2)[:, pair],
             )
 
         def weave(ap_vt):
@@ -65,7 +70,7 @@ def tile_picked_zfp_gelu_po_kernel(
         w1_rows = w1.rearrange("(p j) c -> p j c", j=PACK)
         nc.sync.dma_start(w1_raw[0][:], w1_rows[:, :, : H // 2])
         nc.sync.dma_start(offs_sb[:], offs)
-        for q in range(4):
+        for q in range(QUADRANTS):
             nc.sync.dma_start(
                 xs[32 * q : 32 * q + 4, :].bitcast(I32), x_scales[0, 4 * q : 4 * q + 4, :].bitcast(I32)
             )
@@ -86,18 +91,12 @@ def tile_picked_zfp_gelu_po_kernel(
         xq_w = tile([P, S], U32, "xq_w")
         nc.vector.tensor_copy(xq_s[:], xs[:].indirect(offs_sb[:]))
 
-        w1_bf = [
-            tile([P, PACK, P // 2, PACK], BF16, "w1_bf0"),
-            tile([P, PACK, P // 2, PACK], BF16, "w1_bf1"),
-        ]
+        w1_bf = [tile([P, PACK, P // 2, PACK], BF16, f"w1_bf{u}") for u in range(2)]
         w1_w = [tile([P, P], U32, f"w1_w{t}") for t in range(PACK)]
         w1_s = shared.tile([P, PACK, P], U8, name="w1_s", align_bytes=64, offset=0)
-        deal(nc.scalar.copy, w1_bf[0], w1_raw[0], 0, P // 2)
+        deal(w1_bf[0][:], w1_raw[0][:])
         for pair in range(2):
-            nc.scalar.copy(
-                w1_bf[1][:, 2 * pair : 2 * pair + 2].rearrange("p b m j -> p m j b"),
-                w1_raw[1][:].rearrange("p j (m a b) -> p a m j b", a=2, b=2)[:, pair],
-            )
+            deal_pair(w1_bf[1][:, 2 * pair : 2 * pair + 2], w1_raw[1][:], pair)
 
         def quantise_w1(u, t):
             cols = slice(u * (P // 2), (u + 1) * (P // 2))
@@ -110,26 +109,28 @@ def tile_picked_zfp_gelu_po_kernel(
         for t in range(PACK):
             quantise_w1(0, t)
         quantise_w1(1, 0)
-        for j0, j1 in PIECES:
+        quantise_w1(1, 1)
+        for j0, j1 in WORD_PIECES:
             nc.vector.tensor_copy(xq_w[:, j0:j1], xw[:].bitcast(U32).indirect(offs_sb[:, j0 // 16 : j1 // 16]))
-        for t in range(1, PACK):
+        for t in range(2, PACK):
             quantise_w1(1, t)
 
         h = [tile([P, S], F32, f"h{t}") for t in range(PACK)]
-        for t in range(PACK):
-            for u, (j0, j1) in enumerate(PIECES if t == 0 else ((0, 256), (256, 512))):
-                js = slice(j0, j1)
-                acc = ps.tile([P, j1 - j0], F32, name=f"acc_h{t}{u}", tag=f"bank{(2 * t + u + (t > 0)) % 8}")
-                nc.tensor.matmul_mx(
-                    out=acc[:],
-                    lhsT=w1_w[t][:].bitcast(FP8X4),
-                    lhsT_scale=w1_s[:, t, :],
-                    rhs=xq_w[:, js].bitcast(FP8X4),
-                    rhs_scale=xq_s[:, js],
-                    start=True,
-                    stop=True,
-                )
-                nc.scalar.activation(h[t][:, js], acc[:], GELU)
+        h_pieces = [(t, WORD_PIECES[0]) for t in (0, 1)] + [(t, piece) for t in (0, 1) for piece in WORD_PIECES[1:]]
+        h_pieces = h_pieces + [(t, piece) for t in (2, 3) for piece in LIST_HALVES]
+        for turn, (t, (j0, j1)) in enumerate(h_pieces):
+            js = slice(j0, j1)
+            acc = ps.tile([P, j1 - j0], F32, name=f"acc_h{turn}", tag=f"bank{turn % BANKS}")
+            nc.tensor.matmul_mx(
+                out=acc[:],
+                lhsT=w1_w[t][:].bitcast(FP8X4),
+                lhsT_scale=w1_s[:, t, :],
+                rhs=xq_w[:, js].bitcast(FP8X4),
+                rhs_scale=xq_s[:, js],
+                start=True,
+                stop=True,
+            )
+            nc.scalar.activation(h[t][:, js], acc[:], GELU)
 
         e_bf = [tile([P, HALF_V, PACK], BF16, f"e_bf{u}") for u in range(2)]
         e_w = tile([P, V], U32, "e_w")
@@ -145,19 +146,22 @@ def tile_picked_zfp_gelu_po_kernel(
         terms = [tile([P, PACK, V], F32, f"term{d}") for d in range(2)]
         for t in range(PACK):
             for d in range(2):
-                nc.vector.tensor_tensor(
-                    terms[d][:, t, :], h[t][:].indirect(pos_sb[d][:]), gate_sb[:, d, :], MULT
-                )
+                neighbours = h[t][:].indirect(pos_sb[d][:])
+                if (t, d) == ON_SCALAR:
+                    picked = tile([P, V], F32, "picked")
+                    nc.scalar.activation(picked[:], neighbours, COPY)
+                    neighbours = picked[:]
+                nc.vector.tensor_tensor(terms[d][:, t, :], neighbours, gate_sb[:, d, :], MULT)
 
-        w3_bf = tile([P, PACK, P, PACK], BF16, "w3_bf", "w1_w3")
+        w3_bf = tile([P, PACK, P, PACK], BF16, "w3_bf")
         w2_bf = [tile([P, 2, P, PACK], BF16, f"w2_bf{pair}") for pair in range(2)]
         w3_w = tile([P, N], U32, "w3_w")
         w3_s = tile([P, N], U8, "w3_s")
         w2_w = tile([P, N], U32, "w2_w")
         w2_s = tile([P, N], U8, "w2_s")
-        deal(nc.scalar.copy, w3_bf, w3_raw, 0, P)
+        deal(w3_bf[:], w3_raw[:])
         for pair in range(2):
-            deal_pair(nc.scalar.copy, w2_bf[pair], w2_raw, pair)
+            deal_pair(w2_bf[pair][:], w2_raw[:], pair)
         nc.vector.quantize_mx(
             out=w3_w[:].bitcast(FP8X4), scales=w3_s[:], in_=w3_bf[:].rearrange("p t m j -> p (t m j)")
         )
@@ -211,21 +215,23 @@ def tile_picked_zfp_gelu_po_kernel(
         out_words = out_1[0].rearrange("p v t -> p (v t)").bitcast(I32)
         for pair in range(2):
             ts = slice(2 * pair, 2 * pair + 2)
-            order = [(u, t) for t in (0, 1) for u in range(2)] if pair == 0 else [(u, t) for u in range(2) for t in (2, 3)]
+            if pair == 0:
+                order = [(u, t) for t in (0, 1) for u in range(2)]
+            else:
+                order = [(u, t) for u in range(2) for t in (2, 3)]
             for u, t in order:
                 vs = slice(u * HALF_V, (u + 1) * HALF_V)
-                if True:
-                    acc = accs[PACK * u + t]
-                    nc.tensor.matmul_mx(
-                        out=acc[:],
-                        lhsT=w2_w[:, t * P : (t + 1) * P].bitcast(FP8X4),
-                        lhsT_scale=w2_s[:, t * P : (t + 1) * P],
-                        rhs=z_w[:, vs].bitcast(FP8X4),
-                        rhs_scale=z_s[:, vs],
-                        start=False,
-                        stop=True,
-                    )
-                    nc.scalar.activation(y[:, t, vs], acc[:], GELU)
+                acc = accs[PACK * u + t]
+                nc.tensor.matmul_mx(
+                    out=acc[:],
+                    lhsT=w2_w[:, t * P : (t + 1) * P].bitcast(FP8X4),
+                    lhsT_scale=w2_s[:, t * P : (t + 1) * P],
+                    rhs=z_w[:, vs].bitcast(FP8X4),
+                    rhs_scale=z_s[:, vs],
+                    start=False,
+                    stop=True,
+                )
+                nc.scalar.activation(y[:, t, vs], acc[:], GELU)
             nc.sync.dma_start(out_rows[:, ts, :], y[:, ts, :])
         pieces = (slice(0, HALF_V), slice(HALF_V, HALF_V + QUARTER_V), slice(HALF_V + QUARTER_V, V))
         for c, cols in enumerate(pieces):
@@ -238,7 +244,7 @@ def tile_picked_zfp_gelu_po_kernel(
             if c != 1:
                 vs = slice(c // 2 * HALF_V, (c // 2 + 1) * HALF_V)
                 nc.sync.dma_start(out_words[:, vs], y_w[:, vs].bitcast(I32))
-        for q in range(4):
+        for q in range(QUADRANTS):
             queue = nc.scalar if q % 2 == 0 else nc.sync
             queue.dma_start(
                 out_2[0, 4 * q : 4 * q + 4, :].bitcast(I32), y_s[32 * q : 32 * q + 4, :].bitcast(I32)

from contextlib import ExitStack

import concourse.mybir as mybir

K, T, S, V, H, N = 512, 1024, 512, 256, 512, 512
FLOPS = 2 * K * H * S + 2 * H * N * V + 2 * K * N * V

F32 = mybir.dt.float32
BF16 = mybir.dt.bfloat16
I32 = mybir.dt.int32
U32 = mybir.dt.uint32
U16 = mybir.dt.uint16
U8 = mybir.dt.uint8
FP8X4 = mybir.dt.float8_e4m3fn_x4
GELU = mybir.ActivationFunctionType.Gelu_apprx_tanh
COPY = mybir.ActivationFunctionType.Copy
MULT = mybir.AluOpType.mult
ADD = mybir.AluOpType.add

P = 128
PACK = 4
HALF_V = V // 2
QUARTER_V = V // 4
QUADRANTS = 4
BANKS = 8
WORD_PIECES = ((0, 128), (128, 384), (384, 512))
ON_SCALAR = (PACK - 1, 1)
LIST_HALVES = ((0, S // 2), (S // 2, S))


def tile_picked_zfp_gelu_po_kernel(
    tc, x_words, x_scales, w1, w2, gate, eT, w3, offs, pos1, pos2, out_0, out_1, out_2
):
    nc = tc.nc
    with ExitStack() as ctx:
        sb = ctx.enter_context(tc.tile_pool(name="sb", bufs=1))
        shared = ctx.enter_context(tc.tile_pool(name="shared", bufs=1))
        ps = ctx.enter_context(tc.psum_pool(name="ps", bufs=1))

        def tile(shape, dtype, name, tag=None):
            return sb.tile(shape, dtype, name=name, tag=tag or name, align_bytes=64)

        def deal(dealt, raw):
            nc.scalar.copy(
                dealt.rearrange("p t m j -> p m j t"),
                raw.rearrange("p j (m t) -> p m j t", t=PACK),
            )

        def deal_pair(dealt, raw, pair):
            nc.scalar.copy(
                dealt.rearrange("p b m j -> p m j b"),
                raw.rearrange("p j (m a b) -> p a m j b", a=2, b=2)[:, pair],
            )

        def weave(ap_vt):
            return ap_vt.rearrange("p (c i) t -> p c t i", i=4)

        def planes(ap_tv):
            return ap_tv.rearrange("p t (c i) -> p c t i", i=4)

        offs_sb = tile([P, S // 16], U16, "offs_sb")
        pos_sb = [tile([P, V // 16], U16, f"pos_sb{d}") for d in range(2)]
        xw = tile([P, T], I32, "xw")
        xs = shared.tile([P, T], U8, name="xs", align_bytes=64, offset=0)
        nc.vector.memset(xs[:].bitcast(I32), 0)
        warm = tile([P, 2], F32, "warm")
        nc.vector.memset(warm[:, 0:1], 0.0)
        nc.scalar.activation(warm[:, 1:2], warm[:, 0:1], GELU)
        w1_raw = [tile([P, PACK, H // 2], F32, f"w1_raw{u}") for u in range(2)]
        w1_rows = w1.rearrange("(p j) c -> p j c", j=PACK)
        nc.sync.dma_start(w1_raw[0][:], w1_rows[:, :, : H // 2])
        nc.sync.dma_start(offs_sb[:], offs)
        for q in range(QUADRANTS):
            nc.sync.dma_start(
                xs[32 * q : 32 * q + 4, :].bitcast(I32), x_scales[0, 4 * q : 4 * q + 4, :].bitcast(I32)
            )
        nc.sync.dma_start(w1_raw[1][:], w1_rows[:, :, H // 2 :])
        nc.sync.dma_start(xw[:], x_words[0].rearrange("p n t -> p (n t)").bitcast(I32))
        e_raw = tile([P, PACK, V], F32, "e_raw")
        nc.sync.dma_start(e_raw[:], eT.rearrange("(p j) v -> p j v", j=PACK))
        gate_sb = tile([P, 2, V], F32, "gate_sb")
        nc.sync.dma_start(gate_sb[:], gate.rearrange("d p v -> p d v"))
        nc.sync.dma_start(pos_sb[0][:], pos1)
        nc.sync.dma_start(pos_sb[1][:], pos2)
        w3_raw = tile([P, PACK, N], F32, "w3_raw")
        nc.sync.dma_start(w3_raw[:], w3.rearrange("(p j) c -> p j c", j=PACK))
        w2_raw = tile([P, PACK, N], F32, "w2_raw")
        nc.sync.dma_start(w2_raw[:], w2.rearrange("(p j) c -> p j c", j=PACK))

        xq_s = tile([P, S], U8, "xq_s")
        xq_w = tile([P, S], U32, "xq_w")
        nc.vector.tensor_copy(xq_s[:], xs[:].indirect(offs_sb[:]))

        w1_bf = [tile([P, PACK, P // 2, PACK], BF16, f"w1_bf{u}") for u in range(2)]
        w1_w = [tile([P, P], U32, f"w1_w{t}") for t in range(PACK)]
        w1_s = shared.tile([P, PACK, P], U8, name="w1_s", align_bytes=64, offset=0)
        deal(w1_bf[0][:], w1_raw[0][:])
        for pair in range(2):
            deal_pair(w1_bf[1][:, 2 * pair : 2 * pair + 2], w1_raw[1][:], pair)

        def quantise_w1(u, t):
            cols = slice(u * (P // 2), (u + 1) * (P // 2))
            nc.vector.quantize_mx(
                out=w1_w[t][:, cols].bitcast(FP8X4),
                scales=w1_s[:, t, cols],
                in_=w1_bf[u][:, t].rearrange("p m j -> p (m j)"),
            )

        for t in range(PACK):
            quantise_w1(0, t)
        quantise_w1(1, 0)
        quantise_w1(1, 1)
        for j0, j1 in WORD_PIECES:
            nc.vector.tensor_copy(xq_w[:, j0:j1], xw[:].bitcast(U32).indirect(offs_sb[:, j0 // 16 : j1 // 16]))
        for t in range(2, PACK):
            quantise_w1(1, t)

        h = [tile([P, S], F32, f"h{t}") for t in range(PACK)]
        h_pieces = [(t, WORD_PIECES[0]) for t in (0, 1)] + [(t, piece) for t in (0, 1) for piece in WORD_PIECES[1:]]
        h_pieces = h_pieces + [(t, piece) for t in (2, 3) for piece in LIST_HALVES]
        for turn, (t, (j0, j1)) in enumerate(h_pieces):
            js = slice(j0, j1)
            acc = ps.tile([P, j1 - j0], F32, name=f"acc_h{turn}", tag=f"bank{turn % BANKS}")
            nc.tensor.matmul_mx(
                out=acc[:],
                lhsT=w1_w[t][:].bitcast(FP8X4),
                lhsT_scale=w1_s[:, t, :],
                rhs=xq_w[:, js].bitcast(FP8X4),
                rhs_scale=xq_s[:, js],
                start=True,
                stop=True,
            )
            nc.scalar.activation(h[t][:, js], acc[:], GELU)

        e_bf = [tile([P, HALF_V, PACK], BF16, f"e_bf{u}") for u in range(2)]
        e_w = tile([P, V], U32, "e_w")
        e_s = tile([P, V], U8, "e_s")
        for u in range(2):
            nc.vector.tensor_copy(weave(e_bf[u][:]), planes(e_raw[:, :, u * HALF_V : (u + 1) * HALF_V]))
        for u in range(2):
            vs = slice(u * HALF_V, (u + 1) * HALF_V)
            nc.vector.quantize_mx(
                out=e_w[:, vs].bitcast(FP8X4), scales=e_s[:, vs], in_=e_bf[u][:].rearrange("p v j -> p (v j)")
            )

        terms = [tile([P, PACK, V], F32, f"term{d}") for d in range(2)]
        for t in range(PACK):
            for d in range(2):
                neighbours = h[t][:].indirect(pos_sb[d][:])
                if (t, d) == ON_SCALAR:
                    picked = tile([P, V], F32, "picked")
                    nc.scalar.activation(picked[:], neighbours, COPY)
                    neighbours = picked[:]
                nc.vector.tensor_tensor(terms[d][:, t, :], neighbours, gate_sb[:, d, :], MULT)

        w3_bf = tile([P, PACK, P, PACK], BF16, "w3_bf")
        w2_bf = [tile([P, 2, P, PACK], BF16, f"w2_bf{pair}") for pair in range(2)]
        w3_w = tile([P, N], U32, "w3_w")
        w3_s = tile([P, N], U8, "w3_s")
        w2_w = tile([P, N], U32, "w2_w")
        w2_s = tile([P, N], U8, "w2_s")
        deal(w3_bf[:], w3_raw[:])
        for pair in range(2):
            deal_pair(w2_bf[pair][:], w2_raw[:], pair)
        nc.vector.quantize_mx(
            out=w3_w[:].bitcast(FP8X4), scales=w3_s[:], in_=w3_bf[:].rearrange("p t m j -> p (t m j)")
        )

        accs = []
        for u in range(2):
            vs = slice(u * HALF_V, (u + 1) * HALF_V)
            for t in range(PACK):
                acc = ps.tile([P, HALF_V], F32, name=f"acc_y{u}{t}", tag=f"bank{PACK * u + t}")
                accs.append(acc)
                nc.tensor.matmul_mx(
                    out=acc[:],
                    lhsT=w3_w[:, t * P : (t + 1) * P].bitcast(FP8X4),
                    lhsT_scale=w3_s[:, t * P : (t + 1) * P],
                    rhs=e_w[:, vs].bitcast(FP8X4),
                    rhs_scale=e_s[:, vs],
                    start=True,
                    stop=False,
                )

        z_bf = tile([P, V, PACK], BF16, "z_bf", "w3_raw")
        z_w = tile([P, V], U32, "z_w")
        z_s = tile([P, V], U8, "z_s")
        for u in range(2):
            vs = slice(u * HALF_V, (u + 1) * HALF_V)
            nc.vector.tensor_tensor(
                weave(z_bf[:, vs, :]), planes(terms[0][:, :, vs]), planes(terms[1][:, :, vs]), ADD
            )

        def quantise_w2(t0, t1):
            ms = slice(t0 * P, t1 * P)
            nc.vector.quantize_mx(
                out=w2_w[:, ms].bitcast(FP8X4),
                scales=w2_s[:, ms],
                in_=w2_bf[t0 // 2][:, t0 % 2 : t0 % 2 + t1 - t0].rearrange("p t m j -> p (t m j)"),
            )

        for u in range(2):
            vs = slice(u * HALF_V, (u + 1) * HALF_V)
            nc.vector.quantize_mx(
                out=z_w[:, vs].bitcast(FP8X4), scales=z_s[:, vs], in_=z_bf[:, vs, :].rearrange("p v t -> p (v t)")
            )
        for t0, t1 in ((0, 1), (1, 2), (2, 4)):
            quantise_w2(t0, t1)

        y = tile([P, PACK, V], F32, "y")
        y_bf = [tile([P, n, PACK], BF16, f"y_bf{c}") for c, n in enumerate((HALF_V, QUARTER_V, QUARTER_V))]
        y_w = tile([P, V], U32, "y_w")
        y_s = tile([P, V], U8, "y_s")
        out_rows = out_0.rearrange("(p t) v -> p t v", t=PACK)
        out_words = out_1[0].rearrange("p v t -> p (v t)").bitcast(I32)
        for pair in range(2):
            ts = slice(2 * pair, 2 * pair + 2)
            if pair == 0:
                order = [(u, t) for t in (0, 1) for u in range(2)]
            else:
                order = [(u, t) for u in range(2) for t in (2, 3)]
            for u, t in order:
                vs = slice(u * HALF_V, (u + 1) * HALF_V)
                acc = accs[PACK * u + t]
                nc.tensor.matmul_mx(
                    out=acc[:],
                    lhsT=w2_w[:, t * P : (t + 1) * P].bitcast(FP8X4),
                    lhsT_scale=w2_s[:, t * P : (t + 1) * P],
                    rhs=z_w[:, vs].bitcast(FP8X4),
                    rhs_scale=z_s[:, vs],
                    start=False,
                    stop=True,
                )
                nc.scalar.activation(y[:, t, vs], acc[:], GELU)
            nc.sync.dma_start(out_rows[:, ts, :], y[:, ts, :])
        pieces = (slice(0, HALF_V), slice(HALF_V, HALF_V + QUARTER_V), slice(HALF_V + QUARTER_V, V))
        for c, cols in enumerate(pieces):
            copy = nc.scalar.copy if c == 1 else nc.vector.tensor_copy
            copy(weave(y_bf[c][:]), planes(y[:, :, cols]))
        for c, cols in enumerate(pieces):
            nc.vector.quantize_mx(
                out=y_w[:, cols].bitcast(FP8X4), scales=y_s[:, cols], in_=y_bf[c][:].rearrange("p v t -> p (v t)")
            )
            if c != 1:
                vs = slice(c // 2 * HALF_V, (c // 2 + 1) * HALF_V)
                nc.sync.dma_start(out_words[:, vs], y_w[:, vs].bitcast(I32))
        for q in range(QUADRANTS):
            queue = nc.scalar if q % 2 == 0 else nc.sync
            queue.dma_start(
                out_2[0, 4 * q : 4 * q + 4, :].bitcast(I32), y_s[32 * q : 32 * q + 4, :].bitcast(I32)
            )
